import numpy as np
import ml_dtypes


def mxq(x, axis, fmt="e4m3"):
    dtype, down = {"e4m3": (ml_dtypes.float8_e4m3fn, 7), "e5m2": (ml_dtypes.float8_e5m2, 14)}[fmt]
    v = np.moveaxis(np.asarray(x, np.float32).astype(ml_dtypes.bfloat16).astype(np.float64), axis, -1)
    blocks = v.reshape(v.shape[:-1] + (-1, 32))
    amax = np.abs(blocks).max(-1, keepdims=True)
    byte = np.maximum(np.where(amax > 0, np.frexp(amax)[1] - 1 + 127, 0) - down, 1)
    scale = np.exp2(byte - 127.0)
    codes = (blocks / scale).astype(np.float32).astype(dtype).astype(np.float64)
    return np.moveaxis((codes * scale).reshape(v.shape), -1, axis)


WIDE = False


def mx_kscale(k):
    if not WIDE:
        return np.ones(k)
    levels = np.array([10, -10, 5, -5, 0])
    if k % 512:
        return np.exp2(np.random.permutation(np.resize(levels, k // 32))).repeat(32)
    a = np.empty((k // 512, 16))
    for p in range(k // 512):
        a[p, :8] = np.random.permutation(np.resize(levels, 8))
        for g in range(8):
            far = levels[np.abs(levels - a[p, g]) >= 10]
            a[p, g + 8] = far[np.random.randint(len(far))]
    return np.exp2(a.ravel()).repeat(32)


BF16 = ml_dtypes.bfloat16


def bf(x):
    return np.asarray(x, np.float32).astype(BF16)


def f64(x):
    return np.asarray(x).astype(np.float64)

def planes(Y):
    n, m = Y.shape
    b = f64(bf(Y)).reshape(n // 32, 32, m)
    amax = np.abs(b).max(1)
    byte = np.clip(np.where(amax > 0, np.frexp(amax)[1] - 1 + 127 - 7, 1), 1, 254)
    codes = (b * np.exp2(127.0 - byte)[:, None, :]).reshape(n, m).astype(np.float32).astype(ml_dtypes.float8_e4m3fn).view(np.uint8)
    words = codes.reshape(n // 512, 128, 4, m).transpose(0, 1, 3, 2)
    return np.ascontiguousarray(words), np.ascontiguousarray(byte.astype(np.uint8).reshape(n // 512, 16, m))


R, F, L = 4096, 512, 1024

def setup_inputs():
    s = mx_kscale(F)
    t = mx_kscale(R)
    centre = 0.5 * np.random.randn(F)
    x = centre + np.random.randn(R, F)
    noise = np.random.randn(F, F)
    prec = 1.1 * np.eye(F) + 0.5 * (noise + noise.T) / np.sqrt(2 * F)
    groups = np.random.randint(-1, 2, (R, L)) / np.sqrt(R)
    weight = np.exp(0.3 * np.random.randn(R))
    return {
        "x": bf(x * s),
        "centre": bf(centre * s),
        "prec": bf(prec / s[:, None] / s[None, :]),
        "weight": bf(weight * t),
        "groups": bf(groups / t[:, None]),
        "comparison": bf(np.exp(0.3 * np.random.randn(L))),
        "penalty": bf(0.6 * np.exp(0.8 * np.random.randn(F))),
    }

def reference(x, centre, prec, weight, groups, comparison, penalty):
    x, centre, prec, weight = f64(x), f64(centre), f64(prec), f64(weight)
    groups, comparison, penalty = f64(groups), f64(comparison), f64(penalty)
    D = x - centre[None, :]
    Q = mxq(D, 1, "e4m3") @ mxq(prec, 0, "e4m3")
    C = Q * x * weight[:, None]
    S = mxq(groups, 0, "e4m3").T @ mxq(C, 0, "e4m3")
    y = S * penalty[None, :] * comparison[:, None]
    Y = y.T
    words, scales = planes(Y)
    return y, words, scales

@@ -1,0 +1,453 @@
+from contextlib import ExitStack
+
+import concourse.mybir as mybir
+from concourse.masks import make_identity
+
+R, F, L = 4096, 512, 1024
+FLOPS = 2 * R * F * F + 2 * R * F * L
+
+F32 = mybir.dt.float32
+BF16 = mybir.dt.bfloat16
+I32 = mybir.dt.int32
+U32 = mybir.dt.uint32
+U8 = mybir.dt.uint8
+FP8X4 = mybir.dt.float8_e4m3fn_x4
+ALU = mybir.AluOpType
+ACT = mybir.ActivationFunctionType
+
+P = 128
+PACK = 4
+K_PASS = P * PACK
+PASSES = R // K_PASS
+TILES = L // P
+HALF = L // 2
+RUN = 4
+X_BUFS = 4
+G_BUFS = 3
+
+
+def tile_weighted_group_scale_gradient_h3_kernel(
+    tc, x, centre, prec, weight, groups, comparison, penalty, out_0, out_1, out_2
+):
+    nc = tc.nc
+    with ExitStack() as ctx:
+        sb = ctx.enter_context(tc.tile_pool(name="sb", bufs=1))
+        ps = ctx.enter_context(tc.psum_pool(name="ps", bufs=1))
+
+        def tiles(name, count, shape, dtype):
+            return [sb.tile(shape, dtype, name="%s%d" % (name, i), align_bytes=64) for i in range(count)]
+
+        def one(name, shape, dtype):
+            return tiles(name, 1, shape, dtype)[0]
+
+        bank = [ps.tile([P, 512], F32, name="bank%d" % i) for i in range(8)]
+        turn_banks, q_banks = bank[4:6], bank[6:8]
+
+        ident_f32 = one("ident_f32", [P, P], F32)
+        ident_bf16 = one("ident_bf16", [P, P], BF16)
+        rows = one("rows", [P, K_PASS], BF16)
+        warm = one("warm", [P, 8], F32)
+        centre_sb = one("centre_sb", [P, PACK], BF16)
+        weight_sb = one("weight_sb", [P, PASSES, PACK], F32)
+        comparison_sb = one("comparison_sb", [P, TILES], F32)
+        penalty_sb = one("penalty_sb", [P, F], BF16)
+        prec_raw = one("prec_raw", [P, PACK, F], BF16)
+        prec_il = one("prec_il", [P, F, PACK], BF16)
+        prec_codes = one("prec_codes", [P, F], U32)
+        prec_scales = one("prec_scales", [P, F], U8)
+        prec_own = one("prec_own", [P, F], U32)
+        x_sb = tiles("x_sb", X_BUFS, [P, PACK, F], BF16)
+        ring = tiles("ring", 3, [P, PACK * F], F32)
+        d_il = tiles("d_il", 2, [P, K_PASS, PACK], BF16)
+        d_codes = tiles("d_codes", 2, [P, K_PASS], U32)
+        d_scales = tiles("d_scales", 2, [P, K_PASS], U8)
+        c_codes = tiles("c_codes", PASSES, [P, F], U32)
+        c_scales = tiles("c_scales", PASSES, [P, F], U8)
+        g_raw = tiles("g_raw", G_BUFS, [P, PACK, L], BF16)
+        ge_il = tiles("ge_il", 2, [P, HALF, PACK], BF16)
+        ge_codes = tiles("ge_codes", 2, [P, HALF], U32)
+        ge_scales = tiles("ge_scales", 2, [P, HALF], U8)
+        gl_il = one("gl_il", [P, TILES // 2, PASSES, P, PACK], BF16)
+        gl_codes = one("gl_codes", [P, TILES // 2, PASSES * P], U32)
+        gl_scales = one("gl_scales", [P, TILES // 2, PASSES * P], U8)
+        y_sb = tiles("y_sb", 4, [P, F], F32)
+        y_bf = tiles("y_bf", 4, [P, F], BF16)
+        y_il = tiles("y_il", 3, [P, 2 * P, PACK], BF16)
+        y_codes = one("y_codes", [P, L], U32)
+        y_scales = one("y_scales", [P, L], U8)
+
+        x_hbm = x.rearrange("(g p t) f -> g p t f", p=P, t=PACK)
+        groups_hbm = groups.rearrange("(g p t) l -> g p t l", p=P, t=PACK)
+        words_hbm = out_1.rearrange("g p m t -> p (g m t)").bitcast(I32)
+        scales_hbm = out_2.rearrange("g q m -> (g q) m").bitcast(I32)
+
+        def flat(t):
+            return t.rearrange("p w t -> p (w t)")
+
+        def quantize(codes, scales, grouped):
+            nc.vector.quantize_mx(out=codes.bitcast(FP8X4), scales=scales, in_=flat(grouped))
+
+        def copy_on(engine, out, in_):
+            if engine == "vector":
+                nc.vector.tensor_copy(out=out, in_=in_)
+            else:
+                nc.scalar.copy(out=out, in_=in_)
+
+        def interleave(engine, grouped, raw):
+            copy_on(
+                engine,
+                grouped.rearrange("p (c i) t -> p c t i", i=RUN),
+                raw.rearrange("p t (c i) -> p c t i", i=RUN),
+            )
+
+        def mx(out, l_codes, l_scales, r_codes, r_scales, start, stop):
+            nc.tensor.matmul_mx(
+                out=out,
+                lhsT=l_codes.bitcast(FP8X4),
+                lhsT_scale=l_scales,
+                rhs=r_codes.bitcast(FP8X4),
+                rhs_scale=r_scales,
+                start=start,
+                stop=stop,
+            )
+
+        def cols(i, width=P):
+            return slice(i * width, (i + 1) * width)
+
+        def load_x(g, lo=0, hi=PACK):
+            nc.sync.dma_start(out=x_sb[g % X_BUFS][:, lo:hi, :], in_=x_hbm[g, :, lo:hi, :])
+
+        def load_prec():
+            nc.sync.dma_start(out=prec_raw[:], in_=prec.rearrange("(p t) j -> p t j", t=PACK))
+
+        def load_groups(g):
+            nc.sync.dma_start(out=g_raw[g % G_BUFS][:], in_=groups_hbm[g])
+
+        def load_penalty():
+            nc.sync.dma_start(out=penalty_sb[:], in_=penalty.partition_broadcast(P))
+
+        def constants():
+            nc.gpsimd.memset(rows[:].bitcast(I32), 0)
+            make_identity(nc, ident_f32[:])
+            make_identity(nc, ident_bf16[:])
+            nc.gpsimd.memset(prec_own[:].bitcast(I32), 0)
+            nc.vector.memset(warm[:], 0.0)
+            nc.scalar.dma_start(out=centre_sb[:], in_=centre.rearrange("(p t) -> p t", t=PACK))
+            nc.scalar.dma_start(out=rows[0:PASSES, :], in_=weight.rearrange("(g k) -> g k", k=K_PASS))
+            nc.scalar.dma_start(
+                out=rows[PASSES : PASSES + TILES, 0:P], in_=comparison.rearrange("(m p) -> m p", p=P)
+            )
+            nc.scalar.activation(out=warm[:, 0:1], in_=warm[:, 1:2], func=ACT.Copy, scale=warm[:, 2:3])
+
+        def turn_rows():
+            words = rows[:].bitcast(F32)
+            for u in range(2):
+                nc.tensor.transpose(bank[0][:, cols(u)], words[:, u : 2 * P : 2], ident_f32[:])
+            nc.tensor.transpose(bank[0][:, 2 * P : 2 * P + P // 2].bitcast(BF16), rows[:, 0:P], ident_bf16[:])
+
+        def spread_rows():
+            halves = bank[0][:, 0 : 2 * P].bitcast(BF16).rearrange("p (u r e) -> p r u e", u=2, e=2)
+            nc.vector.tensor_copy(
+                out=weight_sb[:].rearrange("p g (u e) -> p g u e", e=2), in_=halves[:, 0:PASSES, :, :]
+            )
+            turned = bank[0][:, 2 * P : 2 * P + P // 2].bitcast(BF16)
+            nc.vector.tensor_copy(out=comparison_sb[:], in_=turned[:, PASSES : PASSES + TILES])
+
+        def interleave_prec(engine, half):
+            interleave(engine, prec_il[:, cols(half, F // 2), :], prec_raw[:, :, cols(half, F // 2)])
+
+        def quantize_prec():
+            quantize(prec_codes[:], prec_scales[:], prec_il[:])
+
+        def own_lane(codes):
+            return codes[:].bitcast(U8).rearrange("p (a r) -> p a r", r=4 * PACK)[:, :, 0 : 4 * PACK : PACK + 1]
+
+        def split_prec():
+            nc.vector.tensor_copy(out=own_lane(prec_own), in_=own_lane(prec_codes))
+
+        def clear_lanes():
+            nc.gpsimd.memset(own_lane(prec_codes), 0)
+
+        def xw(g):
+            return ring[(g + 1) % 3][:].rearrange("p (t f) -> p t f", t=PACK)
+
+        def c_il(g):
+            return ring[g % 3][:, 0 : PACK * F // 2].bitcast(BF16).rearrange("p (f t) -> p f t", t=PACK)
+
+        def turn_x(g, half):
+            words = x_sb[g % X_BUFS][:].rearrange("p t f -> p (t f)").bitcast(F32)
+            for tt in range(2):
+                first = (2 * half + tt) * (F // 2)
+                for u in range(2):
+                    nc.tensor.transpose(
+                        turn_banks[half][:, cols(2 * u + tt)],
+                        words[:, first + u : first + F // 2 : 2],
+                        ident_f32[:],
+                    )
+
+        def centre_x(g, half):
+            nc.vector.tensor_tensor(
+                out=d_il[g % 2][:, cols(half, 2 * P), :].rearrange("p r (u e) -> p r u e", e=2),
+                in0=turn_banks[half][:].bitcast(BF16).rearrange("p (u r e) -> p r u e", u=2, e=2),
+                in1=centre_sb[:].rearrange("p (u e) -> p u e", e=2).unsqueeze(1).to_broadcast([P, 2 * P, 2, 2]),
+                op=ALU.subtract,
+            )
+
+        def quantize_d(g):
+            quantize(d_codes[g % 2][:], d_scales[g % 2][:], d_il[g % 2][:])
+
+        def stage_one(g, c):
+            for t in range(PACK):
+                for part, codes in enumerate((prec_codes, prec_own)):
+                    mx(
+                        q_banks[c % 2][:, cols(t)],
+                        d_codes[g % 2][:, cols(t)],
+                        d_scales[g % 2][:, cols(t)],
+                        codes[:, cols(c)],
+                        prec_scales[:, cols(c)],
+                        part == 0,
+                        part == 1,
+                    )
+
+        def weigh_x(g, engine):
+            for t in range(PACK):
+                out, in_, factor = xw(g)[:, t, :], x_sb[g % X_BUFS][:, t, :], weight_sb[:, g, t : t + 1]
+                if engine == "scalar":
+                    nc.scalar.activation(out=out, in_=in_, func=ACT.Copy, scale=factor)
+                else:
+                    nc.gpsimd.tensor_scalar(
+                        out=out, in0=in_, scalar1=factor, scalar2=0.0, op0=ALU.mult, op1=ALU.add
+                    )
+
+        def make_c(g, c):
+            nc.vector.tensor_tensor(
+                out=c_il(g)[:, cols(c), :].rearrange("p (c i) t -> p c t i", i=RUN),
+                in0=q_banks[c % 2][:].rearrange("p (t c i) -> p c t i", t=PACK, i=RUN),
+                in1=xw(g)[:, :, cols(c)].rearrange("p t (c i) -> p c t i", i=RUN),
+                op=ALU.mult,
+            )
+
+        def quantize_c(g):
+            quantize(c_codes[g][:], c_scales[g][:], c_il(g))
+
+        def interleave_early(g):
+            interleave("scalar", ge_il[g % 2][:], g_raw[g % G_BUFS][:, :, 0:HALF])
+
+        def interleave_late(g):
+            nc.scalar.copy(
+                out=gl_il[:, :, g, :, :].rearrange("p m (c i) t -> p m c t i", i=RUN),
+                in_=g_raw[g % G_BUFS][:, :, HALF:L].rearrange("p t (m c i) -> p m c t i", c=P // RUN, i=RUN),
+            )
+
+        def quantize_early(g):
+            quantize(ge_codes[g % 2][:], ge_scales[g % 2][:], ge_il[g % 2][:])
+
+        def quantize_late(m, g0, g1):
+            span = slice(g0 * P, g1 * P)
+            late = m - TILES // 2
+            quantize(
+                gl_codes[:, late, span],
+                gl_scales[:, late, span],
+                gl_il[:, late, g0:g1, :, :].rearrange("p g l t -> p (g l) t"),
+            )
+
+        def stage_two(m, g0, g1):
+            for g in range(g0, g1):
+                if m < TILES // 2:
+                    codes, scales = ge_codes[g % 2][:, cols(m)], ge_scales[g % 2][:, cols(m)]
+                else:
+                    codes, scales = gl_codes[:, m - TILES // 2, cols(g)], gl_scales[:, m - TILES // 2, cols(g)]
+                mx(bank[m][:], codes, scales, c_codes[g][:], c_scales[g][:], g == 0, g == PASSES - 1)
+
+        def scale_out(m):
+            nc.vector.scalar_tensor_tensor(
+                out=y_sb[m % 4][:],
+                in0=bank[m][:],
+                scalar=comparison_sb[:, m : m + 1],
+                in1=penalty_sb[:],
+                op0=ALU.mult,
+                op1=ALU.mult,
+            )
+            nc.sync.dma_start(out=out_0[cols(m), :], in_=y_sb[m % 4][:])
+
+        def scale_out_rounded(m):
+            nc.vector.scalar_tensor_tensor(
+                out=y_bf[m % 4][:],
+                in0=bank[m][:],
+                scalar=comparison_sb[:, m : m + 1],
+                in1=penalty_sb[:],
+                op0=ALU.mult,
+                op1=ALU.mult,
+            )
+
+        def round_y(engine, m):
+            copy_on(engine, y_bf[m % 4][:], y_sb[m % 4][:])
+
+        def turn_y(ms, b):
+            for i, m in enumerate(ms):
+                words = y_bf[m % 4][:].bitcast(F32)
+                for u in range(2):
+                    nc.tensor.transpose(bank[b][:, cols(2 * u + i)], words[:, u : F // 2 : 2], ident_f32[:])
+
+        def gather_y(engine, ms, b, slot):
+            width = len(ms) * P
+            copy_on(
+                engine,
+                flat(y_il[slot][:, 0:width, :]).bitcast(F32).rearrange("p (r u) -> p r u", u=2),
+                bank[b][:].rearrange("p (u r) -> p r u", u=2)[:, 0:width, :],
+            )
+
+        def quantize_y(ms, slot):
+            width = len(ms) * P
+            span = slice(ms[0] * P, ms[0] * P + width)
+            quantize(y_codes[:, span], y_scales[:, span], y_il[slot][:, 0:width, :])
+
+        def store_planes(m0, m1, second_queue):
+            span = slice(m0 * P, m1 * P)
+            nc.sync.dma_start(out=words_hbm[:, span], in_=y_codes[:, span].bitcast(I32))
+            scale_words = y_scales[:].bitcast(I32)
+            word_span = slice(m0 * P // 4, m1 * P // 4)
+            for quad in range(4):
+                queue = nc.sync if quad % 2 == 0 else second_queue
+                queue.dma_start(
+                    out=scales_hbm[4 * quad : 4 * quad + 4, word_span],
+                    in_=scale_words[32 * quad : 32 * quad + 4, word_span],
+                )
+
+        ctx.enter_context(tc.manual_schedule())
+        load_x(0, 0, 2)
+        load_prec()
+        load_x(0, 2, 4)
+        constants()
+        load_x(1)
+        load_groups(0)
+        load_x(2)
+        load_groups(1)
+        load_x(3)
+        load_groups(2)
+
+        turn_x(0, 0)
+        turn_rows()
+        turn_x(0, 1)
+        centre_x(0, 0)
+        interleave_prec("scalar", 1)
+        interleave_prec("vector", 0)
+        spread_rows()
+        weigh_x(0, "scalar")
+        turn_x(1, 0)
+        quantize_prec()
+        centre_x(0, 1)
+        turn_x(1, 1)
+        split_prec()
+        clear_lanes()
+        quantize_d(0)
+        stage_one(0, 0)
+        stage_one(0, 1)
+        interleave_early(0)
+
+        last = PASSES - 1
+        for s in range(last):
+            if s > 0:
+                stage_two(0, s - 1, s)
+                stage_two(1, s - 1, s)
+            weigh_x(s + 1, "gpsimd")
+            if s == 0:
+                centre_x(1, 0)
+                centre_x(1, 1)
+            make_c(s, 0)
+            stage_one(s, 2)
+            if s > 0:
+                stage_two(2, s - 1, s)
+                centre_x(s + 1, 0)
+            make_c(s, 1)
+            stage_one(s, 3)
+            if s > 0:
+                centre_x(s + 1, 1)
+            if s + 2 <= last:
+                turn_x(s + 2, 0)
+                turn_x(s + 2, 1)
+            else:
+                stage_two(4, 0, 4)
+            if s > 0:
+                stage_two(3, s - 1, s)
+            make_c(s, 2)
+            make_c(s, 3)
+            quantize_d(s + 1)
+            stage_one(s + 1, 0)
+            stage_one(s + 1, 1)
+            interleave_late(s)
+            interleave_early(s + 1)
+            if s == last - 2:
+                quantize_late(4, 0, 4)
+            if s == last - 1:
+                quantize_late(5, 0, 4)
+            quantize_early(s)
+            quantize_c(s)
+            if s + 4 <= last:
+                load_x(s + 4)
+            if s + 3 <= last:
+                load_groups(s + 3)
+            if s == 4:
+                load_penalty()
+
+        interleave_late(last)
+        stage_two(0, last - 1, last)
+        make_c(last, 0)
+        stage_one(last, 2)
+        stage_two(1, last - 1, last)
+        make_c(last, 1)
+        stage_one(last, 3)
+        quantize_early(last)
+        stage_two(2, last - 1, last)
+        stage_two(3, last - 1, last)
+        make_c(last, 2)
+        make_c(last, 3)
+        stage_two(5, 0, 4)
+        quantize_late(6, 0, 4)
+        quantize_c(last)
+        for m in range(4):
+            stage_two(m, last, PASSES)
+        quantize_late(4, 4, 8)
+        stage_two(6, 0, 4)
+        stage_two(4, 4, 8)
+        scale_out(0)
+        round_y("scalar", 0)
+        quantize_late(5, 4, 8)
+        scale_out(1)
+        round_y("scalar", 1)
+        stage_two(5, 4, 8)
+        quantize_late(6, 4, 8)
+        scale_out(2)
+        round_y("scalar", 2)
+        quantize_late(7, 0, 4)
+        scale_out(3)
+        round_y("scalar", 3)
+        turn_y([0, 1], 0)
+        stage_two(6, 4, 8)
+        quantize_late(7, 4, 8)
+        gather_y("scalar", [0, 1], 0, 0)
+        scale_out(4)
+        round_y("scalar", 4)
+        stage_two(7, 0, 4)
+        turn_y([2, 3], 1)
+        scale_out(5)
+        round_y("vector", 5)
+        quantize_y([0, 1], 0)
+        gather_y("scalar", [2, 3], 1, 1)
+        scale_out(6)
+        round_y("scalar", 6)
+        stage_two(7, 4, 8)
+        turn_y([4, 5], 2)
+        turn_y([6], 3)
+        quantize_y([2, 3], 1)
+        store_planes(0, 4, nc.sync)
+        scale_out_rounded(7)
+        gather_y("scalar", [4, 5], 2, 0)
+        turn_y([7], 0)
+        scale_out(7)
+        gather_y("scalar", [6], 3, 1)
+        quantize_y([4, 5], 0)
+        gather_y("scalar", [7], 0, 2)
+        quantize_y([6], 1)
+        quantize_y([7], 2)
+        store_planes(4, 8, nc.scalar)

@@ -221,9 +221,9 @@ def tile_weighted_group_scale_gradient_h3_kernel(
 
         def make_c(g, c):
             nc.vector.tensor_tensor(
-                out=c_il(g)[:, cols(c), :].rearrange("p (c i) t -> p c t i", i=RUN),
-                in0=q_banks[c % 2][:].rearrange("p (t c i) -> p c t i", t=PACK, i=RUN),
-                in1=xw(g)[:, :, cols(c)].rearrange("p t (c i) -> p c t i", i=RUN),
+                out=c_il(g)[:, cols(c), :].rearrange("p (c i) t -> p c t i", i=2),
+                in0=q_banks[c % 2][:].rearrange("p (t c i) -> p c t i", t=PACK, i=2),
+                in1=xw(g)[:, :, cols(c)].rearrange("p t (c i) -> p c t i", i=2),
                 op=ALU.mult,
             )
 
@@ -315,8 +315,8 @@ def tile_weighted_group_scale_gradient_h3_kernel(
                 )
 
         ctx.enter_context(tc.manual_schedule())
-        load_x(0, 0, 2)
         load_prec()
+        load_x(0, 0, 2)
         load_x(0, 2, 4)
         constants()
         load_x(1)
@@ -326,62 +326,91 @@ def tile_weighted_group_scale_gradient_h3_kernel(
         load_x(3)
         load_groups(2)
 
+        interleave_prec("scalar", 1)
+        interleave_prec("vector", 0)
         turn_x(0, 0)
         turn_rows()
         turn_x(0, 1)
         centre_x(0, 0)
-        interleave_prec("scalar", 1)
-        interleave_prec("vector", 0)
+        quantize_prec()
         spread_rows()
         weigh_x(0, "scalar")
         turn_x(1, 0)
-        quantize_prec()
-        centre_x(0, 1)
-        turn_x(1, 1)
         split_prec()
         clear_lanes()
+        centre_x(0, 1)
+        turn_x(1, 1)
+        centre_x(1, 0)
         quantize_d(0)
         stage_one(0, 0)
         stage_one(0, 1)
+        centre_x(1, 1)
         interleave_early(0)
 
         last = PASSES - 1
-        for s in range(last):
+        for s in range(PASSES):
+            ahead = s + 2
+            if s == 0:
+                turn_x(2, 0)
+                turn_x(2, 1)
             if s > 0:
                 stage_two(0, s - 1, s)
                 stage_two(1, s - 1, s)
-            weigh_x(s + 1, "gpsimd")
-            if s == 0:
-                centre_x(1, 0)
-                centre_x(1, 1)
+            if s < last:
+                weigh_x(s + 1, "gpsimd" if ahead <= last else "scalar")
             make_c(s, 0)
             stage_one(s, 2)
-            if s > 0:
-                stage_two(2, s - 1, s)
-                centre_x(s + 1, 0)
+            if s == 0:
+                quantize_d(1)
+            elif ahead <= last:
+                centre_x(ahead, 0)
+            elif s == last - 1:
+                quantize_late(5, 0, 4)
             make_c(s, 1)
             stage_one(s, 3)
-            if s > 0:
-                centre_x(s + 1, 1)
-            if s + 2 <= last:
-                turn_x(s + 2, 0)
-                turn_x(s + 2, 1)
+            if s == 0:
+                centre_x(ahead, 0)
+            elif ahead <= last:
+                centre_x(ahead, 1)
+            elif s == last - 1:
+                quantize_late(6, 0, 4)
             else:
-                stage_two(4, 0, 4)
+                quantize_early(last)
             if s > 0:
+                stage_two(2, s - 1, s)
                 stage_two(3, s - 1, s)
             make_c(s, 2)
+            if s < last:
+                stage_one(s + 1, 0)
+            if s == 0:
+                centre_x(ahead, 1)
             make_c(s, 3)
-            quantize_d(s + 1)
-            stage_one(s + 1, 0)
-            stage_one(s + 1, 1)
-            interleave_late(s)
-            interleave_early(s + 1)
+            if s < last:
+                stage_one(s + 1, 1)
+            if ahead + 1 <= last:
+                turn_x(ahead + 1, 0)
+                turn_x(ahead + 1, 1)
             if s == last - 2:
-                quantize_late(4, 0, 4)
+                stage_two(4, 0, 4)
             if s == last - 1:
-                quantize_late(5, 0, 4)
-            quantize_early(s)
+                stage_two(5, 0, 4)
+            if s == last:
+                stage_two(6, 0, 4)
+            if s == last - 1:
+                interleave_early(s + 1)
+                interleave_late(s)
+            else:
+                interleave_late(s)
+                if s < last:
+                    interleave_early(s + 1)
+            if s < last:
+                quantize_early(s)
+            if ahead <= last:
+                quantize_d(ahead)
+            else:
+                quantize_late(7, 2 * (s - 6), 2 * (s - 5))
+            if s == last - 3:
+                quantize_late(4, 0, 4)
             quantize_c(s)
             if s + 4 <= last:
                 load_x(s + 4)
@@ -390,64 +419,44 @@ def tile_weighted_group_scale_gradient_h3_kernel(
             if s == 4:
                 load_penalty()
 
-        interleave_late(last)
-        stage_two(0, last - 1, last)
-        make_c(last, 0)
-        stage_one(last, 2)
-        stage_two(1, last - 1, last)
-        make_c(last, 1)
-        stage_one(last, 3)
-        quantize_early(last)
-        stage_two(2, last - 1, last)
-        stage_two(3, last - 1, last)
-        make_c(last, 2)
-        make_c(last, 3)
-        stage_two(5, 0, 4)
-        quantize_late(6, 0, 4)
-        quantize_c(last)
         for m in range(4):
             stage_two(m, last, PASSES)
-        quantize_late(4, 4, 8)
-        stage_two(6, 0, 4)
-        stage_two(4, 4, 8)
+        stage_two(7, 0, 4)
         scale_out(0)
         round_y("scalar", 0)
-        quantize_late(5, 4, 8)
+        quantize_late(4, 4, 8)
+        stage_two(4, 4, 8)
         scale_out(1)
         round_y("scalar", 1)
-        stage_two(5, 4, 8)
-        quantize_late(6, 4, 8)
+        quantize_late(5, 4, 8)
         scale_out(2)
         round_y("scalar", 2)
-        quantize_late(7, 0, 4)
+        turn_y([0, 1], 0)
+        stage_two(5, 4, 8)
+        quantize_late(6, 4, 8)
         scale_out(3)
         round_y("scalar", 3)
-        turn_y([0, 1], 0)
-        stage_two(6, 4, 8)
-        quantize_late(7, 4, 8)
         gather_y("scalar", [0, 1], 0, 0)
+        quantize_late(7, 4, 8)
+        stage_two(6, 4, 8)
+        turn_y([2, 3], 1)
         scale_out(4)
         round_y("scalar", 4)
-        stage_two(7, 0, 4)
-        turn_y([2, 3], 1)
         scale_out(5)
-        round_y("vector", 5)
-        quantize_y([0, 1], 0)
+        round_y("scalar", 5)
         gather_y("scalar", [2, 3], 1, 1)
-        scale_out(6)
-        round_y("scalar", 6)
+        quantize_y([0, 1], 0)
         stage_two(7, 4, 8)
-        turn_y([4, 5], 2)
-        turn_y([6], 3)
+        scale_out(6)
         quantize_y([2, 3], 1)
         store_planes(0, 4, nc.sync)
+        round_y("scalar", 6)
+        turn_y([4, 5], 2)
         scale_out_rounded(7)
         gather_y("scalar", [4, 5], 2, 0)
-        turn_y([7], 0)
+        turn_y([6, 7], 3)
         scale_out(7)
-        gather_y("scalar", [6], 3, 1)
         quantize_y([4, 5], 0)
-        gather_y("scalar", [7], 0, 2)
-        quantize_y([6], 1)
-        quantize_y([7], 2)
+        gather_y("scalar", [6, 7], 3, 1)
+        quantize_y([6, 7], 1)
         store_planes(4, 8, nc.scalar)

@@ -41,7 +41,10 @@ def tile_weighted_group_scale_gradient_h3_kernel(
             return tiles(name, 1, shape, dtype)[0]
 
         bank = [ps.tile([P, 512], F32, name="bank%d" % i) for i in range(8)]
-        turn_banks, q_banks = bank[4:6], bank[6:8]
+        turn_banks = bank[4:6]
+
+        def q_bank(g, c):
+            return bank[c] if g == 0 else bank[6 + c % 2]
 
         ident_f32 = one("ident_f32", [P, P], F32)
         ident_bf16 = one("ident_bf16", [P, P], BF16)
@@ -58,26 +61,24 @@ def tile_weighted_group_scale_gradient_h3_kernel(
         prec_own = one("prec_own", [P, F], U32)
         x_sb = tiles("x_sb", X_BUFS, [P, PACK, F], BF16)
         ring = tiles("ring", 3, [P, PACK * F], F32)
-        d_il = tiles("d_il", 2, [P, K_PASS, PACK], BF16)
+        d_tiles = tiles("d_tiles", 2, [P, K_PASS, PACK], BF16)
         d_codes = tiles("d_codes", 2, [P, K_PASS], U32)
         d_scales = tiles("d_scales", 2, [P, K_PASS], U8)
-        c_codes = tiles("c_codes", PASSES, [P, F], U32)
-        c_scales = tiles("c_scales", PASSES, [P, F], U8)
+        ce_codes = tiles("ce_codes", PASSES, [P, F + HALF], U32)
+        ce_scales = tiles("ce_scales", PASSES, [P, F + HALF], U8)
         g_raw = tiles("g_raw", G_BUFS, [P, PACK, L], BF16)
-        ge_il = tiles("ge_il", 2, [P, HALF, PACK], BF16)
-        ge_codes = tiles("ge_codes", 2, [P, HALF], U32)
-        ge_scales = tiles("ge_scales", 2, [P, HALF], U8)
         gl_il = one("gl_il", [P, TILES // 2, PASSES, P, PACK], BF16)
         gl_codes = one("gl_codes", [P, TILES // 2, PASSES * P], U32)
         gl_scales = one("gl_scales", [P, TILES // 2, PASSES * P], U8)
-        y_sb = tiles("y_sb", 4, [P, F], F32)
-        y_bf = tiles("y_bf", 4, [P, F], BF16)
-        y_il = tiles("y_il", 3, [P, 2 * P, PACK], BF16)
+        y_sb = one("y_sb", [P, TILES, F], F32)
+        y_bf = tiles("y_bf", TILES, [P, F], BF16)
+        y_il = tiles("y_il", 2, [P, HALF, PACK], BF16)
         y_codes = one("y_codes", [P, L], U32)
         y_scales = one("y_scales", [P, L], U8)
 
         x_hbm = x.rearrange("(g p t) f -> g p t f", p=P, t=PACK)
         groups_hbm = groups.rearrange("(g p t) l -> g p t l", p=P, t=PACK)
+        y_hbm = out_0.rearrange("(m p) j -> p m j", p=P)
         words_hbm = out_1.rearrange("g p m t -> p (g m t)").bitcast(I32)
         scales_hbm = out_2.rearrange("g q m -> (g q) m").bitcast(I32)
 
@@ -90,6 +91,8 @@ def tile_weighted_group_scale_gradient_h3_kernel(
         def copy_on(engine, out, in_):
             if engine == "vector":
                 nc.vector.tensor_copy(out=out, in_=in_)
+            elif engine == "gpsimd":
+                nc.gpsimd.tensor_scalar(out=out, in0=in_, scalar1=1.0, scalar2=1.0, op0=ALU.mult, op1=ALU.mult)
             else:
                 nc.scalar.copy(out=out, in_=in_)
 
@@ -117,8 +120,9 @@ def tile_weighted_group_scale_gradient_h3_kernel(
         def load_x(g, lo=0, hi=PACK):
             nc.sync.dma_start(out=x_sb[g % X_BUFS][:, lo:hi, :], in_=x_hbm[g, :, lo:hi, :])
 
-        def load_prec():
-            nc.sync.dma_start(out=prec_raw[:], in_=prec.rearrange("(p t) j -> p t j", t=PACK))
+        def load_prec(half):
+            span = cols(half, F // 2)
+            nc.sync.dma_start(out=prec_raw[:, :, span], in_=prec.rearrange("(p t) j -> p t j", t=PACK)[:, :, span])
 
         def load_groups(g):
             nc.sync.dma_start(out=g_raw[g % G_BUFS][:], in_=groups_hbm[g])
@@ -142,15 +146,15 @@ def tile_weighted_group_scale_gradient_h3_kernel(
         def turn_rows():
             words = rows[:].bitcast(F32)
             for u in range(2):
-                nc.tensor.transpose(bank[0][:, cols(u)], words[:, u : 2 * P : 2], ident_f32[:])
-            nc.tensor.transpose(bank[0][:, 2 * P : 2 * P + P // 2].bitcast(BF16), rows[:, 0:P], ident_bf16[:])
+                nc.tensor.transpose(bank[7][:, cols(u)], words[:, u : 2 * P : 2], ident_f32[:])
+            nc.tensor.transpose(bank[7][:, 2 * P : 2 * P + P // 2].bitcast(BF16), rows[:, 0:P], ident_bf16[:])
 
         def spread_rows():
-            halves = bank[0][:, 0 : 2 * P].bitcast(BF16).rearrange("p (u r e) -> p r u e", u=2, e=2)
+            halves = bank[7][:, 0 : 2 * P].bitcast(BF16).rearrange("p (u r e) -> p r u e", u=2, e=2)
             nc.vector.tensor_copy(
                 out=weight_sb[:].rearrange("p g (u e) -> p g u e", e=2), in_=halves[:, 0:PASSES, :, :]
             )
-            turned = bank[0][:, 2 * P : 2 * P + P // 2].bitcast(BF16)
+            turned = bank[7][:, 2 * P : 2 * P + P // 2].bitcast(BF16)
             nc.vector.tensor_copy(out=comparison_sb[:], in_=turned[:, PASSES : PASSES + TILES])
 
         def interleave_prec(engine, half):
@@ -171,8 +175,11 @@ def tile_weighted_group_scale_gradient_h3_kernel(
         def xw(g):
             return ring[(g + 1) % 3][:].rearrange("p (t f) -> p t f", t=PACK)
 
-        def c_il(g):
-            return ring[g % 3][:, 0 : PACK * F // 2].bitcast(BF16).rearrange("p (f t) -> p f t", t=PACK)
+        def ce_il(g):
+            return ring[g % 3][:].bitcast(BF16).rearrange("p (w t) -> p w t", t=PACK)
+
+        def d_il(g):
+            return ce_il(2)[:, 0:K_PASS, :] if g == 0 else d_tiles[g % 2][:]
 
         def turn_x(g, half):
             words = x_sb[g % X_BUFS][:].rearrange("p t f -> p (t f)").bitcast(F32)
@@ -187,20 +194,20 @@ def tile_weighted_group_scale_gradient_h3_kernel(
 
         def centre_x(g, half):
             nc.vector.tensor_tensor(
-                out=d_il[g % 2][:, cols(half, 2 * P), :].rearrange("p r (u e) -> p r u e", e=2),
+                out=d_il(g)[:, cols(half, 2 * P), :].rearrange("p r (u e) -> p r u e", e=2),
                 in0=turn_banks[half][:].bitcast(BF16).rearrange("p (u r e) -> p r u e", u=2, e=2),
                 in1=centre_sb[:].rearrange("p (u e) -> p u e", e=2).unsqueeze(1).to_broadcast([P, 2 * P, 2, 2]),
                 op=ALU.subtract,
             )
 
         def quantize_d(g):
-            quantize(d_codes[g % 2][:], d_scales[g % 2][:], d_il[g % 2][:])
+            quantize(d_codes[g % 2][:], d_scales[g % 2][:], d_il(g))
 
         def stage_one(g, c):
             for t in range(PACK):
                 for part, codes in enumerate((prec_codes, prec_own)):
                     mx(
-                        q_banks[c % 2][:, cols(t)],
+                        q_bank(g, c)[:, cols(t)],
                         d_codes[g % 2][:, cols(t)],
                         d_scales[g % 2][:, cols(t)],
                         codes[:, cols(c)],
@@ -209,8 +216,8 @@ def tile_weighted_group_scale_gradient_h3_kernel(
                         part == 1,
                     )
 
-        def weigh_x(g, engine):
-            for t in range(PACK):
+        def weigh_x(g, engine, t0, t1):
+            for t in range(t0, t1):
                 out, in_, factor = xw(g)[:, t, :], x_sb[g % X_BUFS][:, t, :], weight_sb[:, g, t : t + 1]
                 if engine == "scalar":
                     nc.scalar.activation(out=out, in_=in_, func=ACT.Copy, scale=factor)
@@ -221,26 +228,23 @@ def tile_weighted_group_scale_gradient_h3_kernel(
 
         def make_c(g, c):
             nc.vector.tensor_tensor(
-                out=c_il(g)[:, cols(c), :].rearrange("p (c i) t -> p c t i", i=2),
-                in0=q_banks[c % 2][:].rearrange("p (t c i) -> p c t i", t=PACK, i=2),
+                out=ce_il(g)[:, cols(c), :].rearrange("p (c i) t -> p c t i", i=2),
+                in0=q_bank(g, c)[:].rearrange("p (t c i) -> p c t i", t=PACK, i=2),
                 in1=xw(g)[:, :, cols(c)].rearrange("p t (c i) -> p c t i", i=2),
                 op=ALU.mult,
             )
 
-        def quantize_c(g):
-            quantize(c_codes[g][:], c_scales[g][:], c_il(g))
+        def quantize_ce(g):
+            quantize(ce_codes[g][:], ce_scales[g][:], ce_il(g))
 
         def interleave_early(g):
-            interleave("scalar", ge_il[g % 2][:], g_raw[g % G_BUFS][:, :, 0:HALF])
+            interleave("scalar", ce_il(g)[:, F : F + HALF, :], g_raw[g % G_BUFS][:, :, 0:HALF])
 
         def interleave_late(g):
             nc.scalar.copy(
                 out=gl_il[:, :, g, :, :].rearrange("p m (c i) t -> p m c t i", i=RUN),
                 in_=g_raw[g % G_BUFS][:, :, HALF:L].rearrange("p t (m c i) -> p m c t i", c=P // RUN, i=RUN),
             )
-
-        def quantize_early(g):
-            quantize(ge_codes[g % 2][:], ge_scales[g % 2][:], ge_il[g % 2][:])
 
         def quantize_late(m, g0, g1):
             span = slice(g0 * P, g1 * P)
@@ -254,69 +258,79 @@ def tile_weighted_group_scale_gradient_h3_kernel(
         def stage_two(m, g0, g1):
             for g in range(g0, g1):
                 if m < TILES // 2:
-                    codes, scales = ge_codes[g % 2][:, cols(m)], ge_scales[g % 2][:, cols(m)]
+                    codes, scales = ce_codes[g][:, cols(PACK + m)], ce_scales[g][:, cols(PACK + m)]
                 else:
                     codes, scales = gl_codes[:, m - TILES // 2, cols(g)], gl_scales[:, m - TILES // 2, cols(g)]
-                mx(bank[m][:], codes, scales, c_codes[g][:], c_scales[g][:], g == 0, g == PASSES - 1)
+                mx(bank[m][:], codes, scales, ce_codes[g][:, 0:F], ce_scales[g][:, 0:F], g == 0, g == PASSES - 1)
 
         def scale_out(m):
             nc.vector.scalar_tensor_tensor(
-                out=y_sb[m % 4][:],
+                out=y_sb[:, m, :],
                 in0=bank[m][:],
                 scalar=comparison_sb[:, m : m + 1],
                 in1=penalty_sb[:],
                 op0=ALU.mult,
                 op1=ALU.mult,
             )
-            nc.sync.dma_start(out=out_0[cols(m), :], in_=y_sb[m % 4][:])
+
+        def store_y(m0, m1):
+            nc.sync.dma_start(out=y_hbm[:, m0:m1, :], in_=y_sb[:, m0:m1, :])
 
         def scale_out_rounded(m):
-            nc.vector.scalar_tensor_tensor(
-                out=y_bf[m % 4][:],
-                in0=bank[m][:],
-                scalar=comparison_sb[:, m : m + 1],
-                in1=penalty_sb[:],
-                op0=ALU.mult,
-                op1=ALU.mult,
-            )
+            for u in range(2):
+                nc.vector.scalar_tensor_tensor(
+                    out=y_bf[m][:, cols(u, F // 2)].rearrange("p (q e) -> p q e", e=2),
+                    in0=bank[m][:].rearrange("p (q u e) -> p u q e", u=2, e=2)[:, u, :, :],
+                    scalar=comparison_sb[:, m : m + 1],
+                    in1=penalty_sb[:].rearrange("p (q u e) -> p u q e", u=2, e=2)[:, u, :, :],
+                    op0=ALU.mult,
+                    op1=ALU.mult,
+                )
 
         def round_y(engine, m):
-            copy_on(engine, y_bf[m % 4][:], y_sb[m % 4][:])
+            copy_on(
+                engine,
+                y_bf[m][:].rearrange("p (u q e) -> p u q e", u=2, e=2),
+                y_sb[:, m, :].rearrange("p (q u e) -> p u q e", u=2, e=2),
+            )
 
         def turn_y(ms, b):
             for i, m in enumerate(ms):
-                words = y_bf[m % 4][:].bitcast(F32)
+                words = y_bf[m][:].bitcast(F32)
                 for u in range(2):
-                    nc.tensor.transpose(bank[b][:, cols(2 * u + i)], words[:, u : F // 2 : 2], ident_f32[:])
+                    nc.tensor.transpose(bank[b][:, cols(2 * u + i)], words[:, cols(u)], ident_f32[:])
 
-        def gather_y(engine, ms, b, slot):
+        def gather_y(engine, ms, b):
             width = len(ms) * P
+            first = (ms[0] % 4) * P
             copy_on(
                 engine,
-                flat(y_il[slot][:, 0:width, :]).bitcast(F32).rearrange("p (r u) -> p r u", u=2),
+                flat(y_il[ms[0] // 4][:, first : first + width, :]).bitcast(F32).rearrange("p (r u) -> p r u", u=2),
                 bank[b][:].rearrange("p (u r) -> p r u", u=2)[:, 0:width, :],
             )
 
-        def quantize_y(ms, slot):
+        def quantize_y(ms):
             width = len(ms) * P
+            first = (ms[0] % 4) * P
             span = slice(ms[0] * P, ms[0] * P + width)
-            quantize(y_codes[:, span], y_scales[:, span], y_il[slot][:, 0:width, :])
+            quantize(y_codes[:, span], y_scales[:, span], y_il[ms[0] // 4][:, first : first + width, :])
 
-        def store_planes(m0, m1, second_queue):
+        def store_words(m0, m1):
             span = slice(m0 * P, m1 * P)
             nc.sync.dma_start(out=words_hbm[:, span], in_=y_codes[:, span].bitcast(I32))
+
+        def store_scales():
             scale_words = y_scales[:].bitcast(I32)
-            word_span = slice(m0 * P // 4, m1 * P // 4)
             for quad in range(4):
-                queue = nc.sync if quad % 2 == 0 else second_queue
+                queue = nc.scalar if quad % 2 == 0 else nc.sync
                 queue.dma_start(
-                    out=scales_hbm[4 * quad : 4 * quad + 4, word_span],
-                    in_=scale_words[32 * quad : 32 * quad + 4, word_span],
+                    out=scales_hbm[4 * quad : 4 * quad + 4, :], in_=scale_words[32 * quad : 32 * quad + 4, :]
                 )
 
         ctx.enter_context(tc.manual_schedule())
-        load_prec()
+        load_prec(1)
         load_x(0, 0, 2)
+        load_prec(0)
         load_x(0, 2, 4)
         constants()
         load_x(1)
@@ -326,92 +340,71 @@ def tile_weighted_group_scale_gradient_h3_kernel(
         load_x(3)
         load_groups(2)
 
-        interleave_prec("scalar", 1)
-        interleave_prec("vector", 0)
         turn_x(0, 0)
         turn_rows()
         turn_x(0, 1)
+        interleave_prec("vector", 1)
+        interleave_prec("scalar", 0)
         centre_x(0, 0)
         quantize_prec()
         spread_rows()
-        weigh_x(0, "scalar")
+        weigh_x(0, "scalar", 0, 4)
         turn_x(1, 0)
         split_prec()
         clear_lanes()
         centre_x(0, 1)
         turn_x(1, 1)
-        centre_x(1, 0)
         quantize_d(0)
-        stage_one(0, 0)
-        stage_one(0, 1)
-        centre_x(1, 1)
-        interleave_early(0)
+        centre_x(1, 0)
+        for c in range(4):
+            stage_one(0, c)
 
         last = PASSES - 1
         for s in range(PASSES):
-            ahead = s + 2
-            if s == 0:
-                turn_x(2, 0)
-                turn_x(2, 1)
             if s > 0:
                 stage_two(0, s - 1, s)
                 stage_two(1, s - 1, s)
+            interleave_early(s)
             if s < last:
-                weigh_x(s + 1, "gpsimd" if ahead <= last else "scalar")
+                weigh_x(s + 1, "gpsimd", 0, 3)
+                weigh_x(s + 1, "scalar", 3, 4)
+            interleave_late(s)
+            if s == 0:
+                centre_x(1, 1)
             make_c(s, 0)
-            stage_one(s, 2)
-            if s == 0:
-                quantize_d(1)
-            elif ahead <= last:
-                centre_x(ahead, 0)
-            elif s == last - 1:
-                quantize_late(5, 0, 4)
-            make_c(s, 1)
-            stage_one(s, 3)
-            if s == 0:
-                centre_x(ahead, 0)
-            elif ahead <= last:
-                centre_x(ahead, 1)
-            elif s == last - 1:
-                quantize_late(6, 0, 4)
-            else:
-                quantize_early(last)
             if s > 0:
+                stage_one(s, 2)
                 stage_two(2, s - 1, s)
+            if 0 < s < last:
+                centre_x(s + 1, 0)
+            make_c(s, 1)
+            if s > 0:
+                stage_one(s, 3)
+            if 0 < s < last:
+                centre_x(s + 1, 1)
+            if s == last:
+                quantize_late(6, 0, 4)
+            if s + 2 <= last:
+                turn_x(s + 2, 0)
+                turn_x(s + 2, 1)
+            if s > 0:
                 stage_two(3, s - 1, s)
+            if s == last - 1:
+                stage_two(4, 0, 4)
+            if s == last:
+                stage_two(5, 2, 4)
+                stage_two(4, 4, 6)
             make_c(s, 2)
-            if s < last:
-                stage_one(s + 1, 0)
-            if s == 0:
-                centre_x(ahead, 1)
             make_c(s, 3)
             if s < last:
+                quantize_d(s + 1)
+                stage_one(s + 1, 0)
                 stage_one(s + 1, 1)
-            if ahead + 1 <= last:
-                turn_x(ahead + 1, 0)
-                turn_x(ahead + 1, 1)
-            if s == last - 2:
-                stage_two(4, 0, 4)
             if s == last - 1:
-                stage_two(5, 0, 4)
-            if s == last:
-                stage_two(6, 0, 4)
-            if s == last - 1:
-                interleave_early(s + 1)
-                interleave_late(s)
-            else:
-                interleave_late(s)
-                if s < last:
-                    interleave_early(s + 1)
-            if s < last:
-                quantize_early(s)
-            if ahead <= last:
-                quantize_d(ahead)
-            else:
-                quantize_late(7, 2 * (s - 6), 2 * (s - 5))
-            if s == last - 3:
-                quantize_late(4, 0, 4)
-            quantize_c(s)
+                stage_two(5, 0, 2)
+            if s >= last - 3:
+                quantize_late(*((4, 0, 4), (5, 0, 4), (4, 4, 6), (7, 0, 4))[s - last + 3])
+            quantize_ce(s)
             if s + 4 <= last:
                 load_x(s + 4)
             if s + 3 <= last:
@@ -419,44 +412,49 @@ def tile_weighted_group_scale_gradient_h3_kernel(
             if s == 4:
                 load_penalty()
 
+        stage_two(6, 0, 4)
         for m in range(4):
             stage_two(m, last, PASSES)
-        stage_two(7, 0, 4)
+        quantize_late(4, 6, 8)
+        quantize_late(5, 4, 8)
+        stage_two(4, 6, 8)
+        stage_two(5, 4, 8)
         scale_out(0)
         round_y("scalar", 0)
-        quantize_late(4, 4, 8)
-        stage_two(4, 4, 8)
+        quantize_late(6, 4, 8)
         scale_out(1)
         round_y("scalar", 1)
-        quantize_late(5, 4, 8)
-        scale_out(2)
-        round_y("scalar", 2)
-        turn_y([0, 1], 0)
-        stage_two(5, 4, 8)
-        quantize_late(6, 4, 8)
-        scale_out(3)
-        round_y("scalar", 3)
-        gather_y("scalar", [0, 1], 0, 0)
+        store_y(0, 2)
         quantize_late(7, 4, 8)
         stage_two(6, 4, 8)
-        turn_y([2, 3], 1)
+        turn_y([0, 1], 0)
+        stage_two(7, 0, 8)
+        scale_out(2)
+        round_y("gpsimd", 2)
+        scale_out(3)
+        round_y("scalar", 3)
+        store_y(2, 4)
+        gather_y("scalar", [0, 1], 0)
         scale_out(4)
-        round_y("scalar", 4)
+        round_y("gpsimd", 4)
         scale_out(5)
         round_y("scalar", 5)
-        gather_y("scalar", [2, 3], 1, 1)
-        quantize_y([0, 1], 0)
-        stage_two(7, 4, 8)
+        store_y(4, 6)
         scale_out(6)
-        quantize_y([2, 3], 1)
-        store_planes(0, 4, nc.sync)
-        round_y("scalar", 6)
+        round_y("gpsimd", 6)
+        quantize_y([0, 1])
+        turn_y([2, 3], 1)
         turn_y([4, 5], 2)
         scale_out_rounded(7)
-        gather_y("scalar", [4, 5], 2, 0)
+        gather_y("scalar", [2, 3], 1)
         turn_y([6, 7], 3)
         scale_out(7)
-        quantize_y([4, 5], 0)
-        gather_y("scalar", [6, 7], 3, 1)
-        quantize_y([6, 7], 1)
-        store_planes(4, 8, nc.scalar)
+        store_y(6, 8)
+        gather_y("scalar", [4, 5], 2)
+        quantize_y([2, 3])
+        store_words(0, 4)
+        gather_y("scalar", [6, 7], 3)
+        quantize_y([4, 5])
+        quantize_y([6, 7])
+        store_words(4, 8)
+        store_scales()

@@ -44,7 +44,11 @@ def tile_weighted_group_scale_gradient_h3_kernel(
         turn_banks = bank[4:6]
 
         def q_bank(g, c):
-            return bank[c] if g == 0 else bank[6 + c % 2]
+            if g == 0:
+                return bank[c]
+            if g == PASSES - 2 and c >= 2:
+                return bank[2 + c]
+            return bank[6 + c % 2]
 
         ident_f32 = one("ident_f32", [P, P], F32)
         ident_bf16 = one("ident_bf16", [P, P], BF16)
@@ -67,9 +71,9 @@ def tile_weighted_group_scale_gradient_h3_kernel(
         ce_codes = tiles("ce_codes", PASSES, [P, F + HALF], U32)
         ce_scales = tiles("ce_scales", PASSES, [P, F + HALF], U8)
         g_raw = tiles("g_raw", G_BUFS, [P, PACK, L], BF16)
-        gl_il = one("gl_il", [P, TILES // 2, PASSES, P, PACK], BF16)
-        gl_codes = one("gl_codes", [P, TILES // 2, PASSES * P], U32)
-        gl_scales = one("gl_scales", [P, TILES // 2, PASSES * P], U8)
+        gl_il = tiles("gl_il", 2, [P, TILES // 2, PASSES // 2, P, PACK], BF16)
+        gl_codes = tiles("gl_codes", 2, [P, TILES // 2, PASSES // 2, P], U32)
+        gl_scales = tiles("gl_scales", 2, [P, TILES // 2, PASSES // 2, P], U8)
         y_sb = one("y_sb", [P, TILES, F], F32)
         y_bf = tiles("y_bf", TILES, [P, F], BF16)
         y_il = tiles("y_il", 2, [P, HALF, PACK], BF16)
@@ -242,17 +246,16 @@ def tile_weighted_group_scale_gradient_h3_kernel(
 
         def interleave_late(g):
             nc.scalar.copy(
-                out=gl_il[:, :, g, :, :].rearrange("p m (c i) t -> p m c t i", i=RUN),
+                out=gl_il[g // 4][:, :, g % 4, :, :].rearrange("p m (c i) t -> p m c t i", i=RUN),
                 in_=g_raw[g % G_BUFS][:, :, HALF:L].rearrange("p t (m c i) -> p m c t i", c=P // RUN, i=RUN),
             )
 
-        def quantize_late(m, g0, g1):
-            span = slice(g0 * P, g1 * P)
-            late = m - TILES // 2
+        def quantize_late(m0, m1, half):
+            late = slice(m0 - TILES // 2, m1 - TILES // 2)
             quantize(
-                gl_codes[:, late, span],
-                gl_scales[:, late, span],
-                gl_il[:, late, g0:g1, :, :].rearrange("p g l t -> p (g l) t"),
+                gl_codes[half][:, late, :, :].rearrange("p m g l -> p (m g l)"),
+                gl_scales[half][:, late, :, :].rearrange("p m g l -> p (m g l)"),
+                gl_il[half][:, late, :, :, :].rearrange("p m g l t -> p (m g l) t"),
             )
 
         def stage_two(m, g0, g1):
@@ -260,7 +263,8 @@ def tile_weighted_group_scale_gradient_h3_kernel(
                 if m < TILES // 2:
                     codes, scales = ce_codes[g][:, cols(PACK + m)], ce_scales[g][:, cols(PACK + m)]
                 else:
-                    codes, scales = gl_codes[:, m - TILES // 2, cols(g)], gl_scales[:, m - TILES // 2, cols(g)]
+                    late = m - TILES // 2
+                    codes, scales = gl_codes[g // 4][:, late, g % 4, :], gl_scales[g // 4][:, late, g % 4, :]
                 mx(bank[m][:], codes, scales, ce_codes[g][:, 0:F], ce_scales[g][:, 0:F], g == 0, g == PASSES - 1)
 
         def scale_out(m):
@@ -356,55 +360,24 @@ def tile_weighted_group_scale_gradient_h3_kernel(
         turn_x(1, 1)
         quantize_d(0)
         centre_x(1, 0)
-        for c in range(4):
-            stage_one(0, c)
+        centre_x(1, 1)
+        stage_one(0, 0)
+        stage_one(0, 1)
+        turn_x(2, 0)
+        turn_x(2, 1)
+        stage_one(0, 2)
+        stage_one(0, 3)
 
         last = PASSES - 1
-        for s in range(PASSES):
-            if s > 0:
-                stage_two(0, s - 1, s)
-                stage_two(1, s - 1, s)
+
+        def side_work(s):
             interleave_early(s)
             if s < last:
                 weigh_x(s + 1, "gpsimd", 0, 3)
                 weigh_x(s + 1, "scalar", 3, 4)
             interleave_late(s)
-            if s == 0:
-                centre_x(1, 1)
-            make_c(s, 0)
-            if s > 0:
-                stage_one(s, 2)
-                stage_two(2, s - 1, s)
-            if 0 < s < last:
-                centre_x(s + 1, 0)
-            make_c(s, 1)
-            if s > 0:
-                stage_one(s, 3)
-            if 0 < s < last:
-                centre_x(s + 1, 1)
-            if s == last:
-                quantize_late(6, 0, 4)
-            if s + 2 <= last:
-                turn_x(s + 2, 0)
-                turn_x(s + 2, 1)
-            if s > 0:
-                stage_two(3, s - 1, s)
-            if s == last - 1:
-                stage_two(4, 0, 4)
-            if s == last:
-                stage_two(5, 2, 4)
-                stage_two(4, 4, 6)
-            make_c(s, 2)
-            make_c(s, 3)
-            if s < last:
-                quantize_d(s + 1)
-                stage_one(s + 1, 0)
-                stage_one(s + 1, 1)
-            if s == last - 1:
-                stage_two(5, 0, 2)
-            if s >= last - 3:
-                quantize_late(*((4, 0, 4), (5, 0, 4), (4, 4, 6), (7, 0, 4))[s - last + 3])
-            quantize_ce(s)
+
+        def next_loads(s):
             if s + 4 <= last:
                 load_x(s + 4)
             if s + 3 <= last:
@@ -412,29 +385,103 @@ def tile_weighted_group_scale_gradient_h3_kernel(
             if s == 4:
                 load_penalty()
 
+        side_work(0)
+        make_c(0, 0)
+        make_c(0, 1)
+        centre_x(2, 0)
+        centre_x(2, 1)
+        quantize_d(1)
+        stage_one(1, 0)
+        stage_one(1, 1)
+        turn_x(3, 0)
+        turn_x(3, 1)
+        make_c(0, 2)
+        make_c(0, 3)
+        quantize_d(2)
+        quantize_ce(0)
+        next_loads(0)
+
+        for s in range(1, last - 1):
+            stage_two(0, s - 1, s)
+            stage_two(1, s - 1, s)
+            side_work(s)
+            make_c(s, 0)
+            make_c(s, 1)
+            stage_one(s, 2)
+            stage_one(s, 3)
+            centre_x(s + 2, 0)
+            centre_x(s + 2, 1)
+            stage_two(2, s - 1, s)
+            stage_two(3, s - 1, s)
+            if s + 3 <= last:
+                turn_x(s + 3, 0)
+                turn_x(s + 3, 1)
+            else:
+                stage_one(s + 1, 2)
+                stage_one(s + 1, 3)
+            make_c(s, 2)
+            make_c(s, 3)
+            stage_one(s + 1, 0)
+            stage_one(s + 1, 1)
+            quantize_d(s + 2)
+            if s == last - 2:
+                quantize_late(4, 5, 0)
+            quantize_ce(s)
+            next_loads(s)
+
+        s = last - 1
+        for m in range(4):
+            stage_two(m, s - 1, s)
+        side_work(s)
+        make_c(s, 0)
+        make_c(s, 1)
+        stage_one(last, 0)
+        stage_one(last, 1)
+        make_c(s, 2)
+        make_c(s, 3)
+        stage_two(4, 0, 4)
+        quantize_late(5, 6, 0)
+        stage_two(5, 0, 4)
+        quantize_ce(s)
+
+        stage_two(0, s, last)
+        stage_two(1, s, last)
+        side_work(last)
+        make_c(last, 0)
+        make_c(last, 1)
+        stage_one(last, 2)
+        stage_one(last, 3)
+        quantize_late(6, 7, 0)
+        stage_two(2, s, last)
+        stage_two(3, s, last)
+        make_c(last, 2)
+        make_c(last, 3)
         stage_two(6, 0, 4)
+        quantize_late(7, 8, 0)
+        stage_two(7, 0, 3)
+        quantize_ce(last)
+
         for m in range(4):
             stage_two(m, last, PASSES)
-        quantize_late(4, 6, 8)
-        quantize_late(5, 4, 8)
-        stage_two(4, 6, 8)
-        stage_two(5, 4, 8)
+        quantize_late(4, 6, 1)
+        stage_two(7, 3, 4)
+        stage_two(4, 4, 8)
         scale_out(0)
         round_y("scalar", 0)
-        quantize_late(6, 4, 8)
         scale_out(1)
         round_y("scalar", 1)
         store_y(0, 2)
-        quantize_late(7, 4, 8)
-        stage_two(6, 4, 8)
+        quantize_late(6, 8, 1)
+        stage_two(5, 4, 8)
         turn_y([0, 1], 0)
-        stage_two(7, 0, 8)
+        stage_two(6, 4, 8)
+        stage_two(7, 4, 8)
         scale_out(2)
         round_y("gpsimd", 2)
+        gather_y("scalar", [0, 1], 0)
         scale_out(3)
         round_y("scalar", 3)
         store_y(2, 4)
-        gather_y("scalar", [0, 1], 0)
         scale_out(4)
         round_y("gpsimd", 4)
         scale_out(5)
@@ -442,16 +489,15 @@ def tile_weighted_group_scale_gradient_h3_kernel(
         store_y(4, 6)
         scale_out(6)
         round_y("gpsimd", 6)
-        quantize_y([0, 1])
         turn_y([2, 3], 1)
-        turn_y([4, 5], 2)
         scale_out_rounded(7)
         gather_y("scalar", [2, 3], 1)
+        turn_y([4, 5], 2)
         turn_y([6, 7], 3)
         scale_out(7)
         store_y(6, 8)
         gather_y("scalar", [4, 5], 2)
-        quantize_y([2, 3])
+        quantize_y([0, 1, 2, 3])
         store_words(0, 4)
         gather_y("scalar", [6, 7], 3)
         quantize_y([4, 5])

@@ -55,6 +55,7 @@ def tile_weighted_group_scale_gradient_h3_kernel(
         rows = one("rows", [P, K_PASS], BF16)
         warm = one("warm", [P, 8], F32)
         centre_sb = one("centre_sb", [P, PACK], BF16)
+        centre_rows = one("centre_rows", [P, 2 * P, PACK], BF16)
         weight_sb = one("weight_sb", [P, PASSES, PACK], F32)
         comparison_sb = one("comparison_sb", [P, TILES], F32)
         penalty_sb = one("penalty_sb", [P, F], BF16)
@@ -147,6 +148,9 @@ def tile_weighted_group_scale_gradient_h3_kernel(
             )
             nc.scalar.activation(out=warm[:, 0:1], in_=warm[:, 1:2], func=ACT.Copy, scale=warm[:, 2:3])
 
+        def repeat_centre():
+            nc.vector.tensor_copy(out=centre_rows[:], in_=centre_sb[:].unsqueeze(1).to_broadcast([P, 2 * P, PACK]))
+
         def turn_rows():
             words = rows[:].bitcast(F32)
             for u in range(2):
@@ -200,7 +204,7 @@ def tile_weighted_group_scale_gradient_h3_kernel(
             nc.vector.tensor_tensor(
                 out=d_il(g)[:, cols(half, 2 * P), :].rearrange("p r (u e) -> p r u e", e=2),
                 in0=turn_banks[half][:].bitcast(BF16).rearrange("p (u r e) -> p r u e", u=2, e=2),
-                in1=centre_sb[:].rearrange("p (u e) -> p u e", e=2).unsqueeze(1).to_broadcast([P, 2 * P, 2, 2]),
+                in1=centre_rows[:].rearrange("p r (u e) -> p r u e", e=2),
                 op=ALU.subtract,
             )
 
@@ -244,10 +248,14 @@ def tile_weighted_group_scale_gradient_h3_kernel(
         def interleave_early(g):
             interleave("scalar", ce_il(g)[:, F : F + HALF, :], g_raw[g % G_BUFS][:, :, 0:HALF])
 
-        def interleave_late(g):
+        def interleave_late(g, m0, m1):
             nc.scalar.copy(
-                out=gl_il[g // 4][:, :, g % 4, :, :].rearrange("p m (c i) t -> p m c t i", i=RUN),
-                in_=g_raw[g % G_BUFS][:, :, HALF:L].rearrange("p t (m c i) -> p m c t i", c=P // RUN, i=RUN),
+                out=gl_il[g // 4][:, m0 - TILES // 2 : m1 - TILES // 2, g % 4, :, :].rearrange(
+                    "p m (c i) t -> p m c t i", i=RUN
+                ),
+                in_=g_raw[g % G_BUFS][:, :, m0 * P : m1 * P].rearrange(
+                    "p t (m c i) -> p m c t i", c=P // RUN, i=RUN
+                ),
             )
 
         def quantize_late(m0, m1, half):
@@ -349,6 +357,7 @@ def tile_weighted_group_scale_gradient_h3_kernel(
         turn_x(0, 1)
         interleave_prec("vector", 1)
         interleave_prec("scalar", 0)
+        repeat_centre()
         centre_x(0, 0)
         quantize_prec()
         spread_rows()
@@ -375,7 +384,7 @@ def tile_weighted_group_scale_gradient_h3_kernel(
             if s < last:
                 weigh_x(s + 1, "gpsimd", 0, 3)
                 weigh_x(s + 1, "scalar", 3, 4)
-            interleave_late(s)
+            interleave_late(s, 4, 8 if s < last - 1 else 6)
 
         def next_loads(s):
             if s + 4 <= last:
@@ -447,6 +456,8 @@ def tile_weighted_group_scale_gradient_h3_kernel(
         stage_two(0, s, last)
         stage_two(1, s, last)
         side_work(last)
+        interleave_late(s, 6, 8)
+        interleave_late(last, 6, 8)
         make_c(last, 0)
         make_c(last, 1)
         stage_one(last, 2)
@@ -489,18 +500,20 @@ def tile_weighted_group_scale_gradient_h3_kernel(
         store_y(4, 6)
         scale_out(6)
         round_y("gpsimd", 6)
+        store_y(6, 7)
         turn_y([2, 3], 1)
         scale_out_rounded(7)
         gather_y("scalar", [2, 3], 1)
         turn_y([4, 5], 2)
         turn_y([6, 7], 3)
         scale_out(7)
-        store_y(6, 8)
+        store_y(7, 8)
         gather_y("scalar", [4, 5], 2)
         quantize_y([0, 1, 2, 3])
         store_words(0, 4)
         gather_y("scalar", [6, 7], 3)
         quantize_y([4, 5])
+        store_words(4, 6)
         quantize_y([6, 7])
-        store_words(4, 8)
+        store_words(6, 8)
         store_scales()

from contextlib import ExitStack

import concourse.mybir as mybir
from concourse.masks import make_identity

R, F, L = 4096, 512, 1024
FLOPS = 2 * R * F * F + 2 * R * F * L

F32 = mybir.dt.float32
BF16 = mybir.dt.bfloat16
I32 = mybir.dt.int32
U32 = mybir.dt.uint32
U8 = mybir.dt.uint8
FP8X4 = mybir.dt.float8_e4m3fn_x4
ALU = mybir.AluOpType
ACT = mybir.ActivationFunctionType

P = 128
PACK = 4
K_PASS = P * PACK
PASSES = R // K_PASS
TILES = L // P
HALF = L // 2
RUN = 4
X_BUFS = 4
G_BUFS = 3


def tile_weighted_group_scale_gradient_h3_kernel(
    tc, x, centre, prec, weight, groups, comparison, penalty, out_0, out_1, out_2
):
    nc = tc.nc
    with ExitStack() as ctx:
        sb = ctx.enter_context(tc.tile_pool(name="sb", bufs=1))
        ps = ctx.enter_context(tc.psum_pool(name="ps", bufs=1))

        def tiles(name, count, shape, dtype):
            return [sb.tile(shape, dtype, name="%s%d" % (name, i), align_bytes=64) for i in range(count)]

        def one(name, shape, dtype):
            return tiles(name, 1, shape, dtype)[0]

        bank = [ps.tile([P, 512], F32, name="bank%d" % i) for i in range(8)]
        turn_banks = bank[4:6]

        def q_bank(g, c):
            if g == 0:
                return bank[c]
            if g == PASSES - 2 and c >= 2:
                return bank[2 + c]
            return bank[6 + c % 2]

        ident_f32 = one("ident_f32", [P, P], F32)
        ident_bf16 = one("ident_bf16", [P, P], BF16)
        rows = one("rows", [P, K_PASS], BF16)
        warm = one("warm", [P, 8], F32)
        centre_sb = one("centre_sb", [P, PACK], BF16)
        centre_rows = one("centre_rows", [P, 2 * P, PACK], BF16)
        weight_sb = one("weight_sb", [P, PASSES, PACK], F32)
        comparison_sb = one("comparison_sb", [P, TILES], F32)
        penalty_sb = one("penalty_sb", [P, F], BF16)
        prec_raw = one("prec_raw", [P, PACK, F], BF16)
        prec_il = one("prec_il", [P, F, PACK], BF16)
        prec_codes = one("prec_codes", [P, F], U32)
        prec_scales = one("prec_scales", [P, F], U8)
        prec_own = one("prec_own", [P, F], U32)
        x_sb = tiles("x_sb", X_BUFS, [P, PACK, F], BF16)
        ring = tiles("ring", 3, [P, PACK * F], F32)
        d_tiles = tiles("d_tiles", 2, [P, K_PASS, PACK], BF16)
        d_codes = tiles("d_codes", 2, [P, K_PASS], U32)
        d_scales = tiles("d_scales", 2, [P, K_PASS], U8)
        ce_codes = tiles("ce_codes", PASSES, [P, F + HALF], U32)
        ce_scales = tiles("ce_scales", PASSES, [P, F + HALF], U8)
        g_raw = tiles("g_raw", G_BUFS, [P, PACK, L], BF16)
        gl_il = tiles("gl_il", 2, [P, TILES // 2, PASSES // 2, P, PACK], BF16)
        gl_codes = tiles("gl_codes", 2, [P, TILES // 2, PASSES // 2, P], U32)
        gl_scales = tiles("gl_scales", 2, [P, TILES // 2, PASSES // 2, P], U8)
        y_sb = one("y_sb", [P, TILES, F], F32)
        y_bf = tiles("y_bf", TILES, [P, F], BF16)
        y_il = tiles("y_il", 2, [P, HALF, PACK], BF16)
        y_codes = one("y_codes", [P, L], U32)
        y_scales = one("y_scales", [P, L], U8)

        x_hbm = x.rearrange("(g p t) f -> g p t f", p=P, t=PACK)
        groups_hbm = groups.rearrange("(g p t) l -> g p t l", p=P, t=PACK)
        y_hbm = out_0.rearrange("(m p) j -> p m j", p=P)
        words_hbm = out_1.rearrange("g p m t -> p (g m t)").bitcast(I32)
        scales_hbm = out_2.rearrange("g q m -> (g q) m").bitcast(I32)

        def flat(t):
            return t.rearrange("p w t -> p (w t)")

        def quantize(codes, scales, grouped):
            nc.vector.quantize_mx(out=codes.bitcast(FP8X4), scales=scales, in_=flat(grouped))

        def copy_on(engine, out, in_):
            if engine == "vector":
                nc.vector.tensor_copy(out=out, in_=in_)
            elif engine == "gpsimd":
                nc.gpsimd.tensor_scalar(out=out, in0=in_, scalar1=1.0, scalar2=1.0, op0=ALU.mult, op1=ALU.mult)
            else:
                nc.scalar.copy(out=out, in_=in_)

        def interleave(engine, grouped, raw):
            copy_on(
                engine,
                grouped.rearrange("p (c i) t -> p c t i", i=RUN),
                raw.rearrange("p t (c i) -> p c t i", i=RUN),
            )

        def mx(out, l_codes, l_scales, r_codes, r_scales, start, stop):
            nc.tensor.matmul_mx(
                out=out,
                lhsT=l_codes.bitcast(FP8X4),
                lhsT_scale=l_scales,
                rhs=r_codes.bitcast(FP8X4),
                rhs_scale=r_scales,
                start=start,
                stop=stop,
            )

        def cols(i, width=P):
            return slice(i * width, (i + 1) * width)

        def load_x(g, lo=0, hi=PACK):
            nc.sync.dma_start(out=x_sb[g % X_BUFS][:, lo:hi, :], in_=x_hbm[g, :, lo:hi, :])

        def load_prec(half):
            span = cols(half, F // 2)
            nc.sync.dma_start(out=prec_raw[:, :, span], in_=prec.rearrange("(p t) j -> p t j", t=PACK)[:, :, span])

        def load_groups(g):
            nc.sync.dma_start(out=g_raw[g % G_BUFS][:], in_=groups_hbm[g])

        def load_penalty():
            nc.sync.dma_start(out=penalty_sb[:], in_=penalty.partition_broadcast(P))

        def constants():
            nc.gpsimd.memset(rows[:].bitcast(I32), 0)
            make_identity(nc, ident_f32[:])
            make_identity(nc, ident_bf16[:])
            nc.gpsimd.memset(prec_own[:].bitcast(I32), 0)
            nc.vector.memset(warm[:], 0.0)
            nc.scalar.dma_start(out=centre_sb[:], in_=centre.rearrange("(p t) -> p t", t=PACK))
            nc.scalar.dma_start(out=rows[0:PASSES, :], in_=weight.rearrange("(g k) -> g k", k=K_PASS))
            nc.scalar.dma_start(
                out=rows[PASSES : PASSES + TILES, 0:P], in_=comparison.rearrange("(m p) -> m p", p=P)
            )
            nc.scalar.activation(out=warm[:, 0:1], in_=warm[:, 1:2], func=ACT.Copy, scale=warm[:, 2:3])

        def repeat_centre():
            nc.vector.tensor_copy(out=centre_rows[:], in_=centre_sb[:].unsqueeze(1).to_broadcast([P, 2 * P, PACK]))

        def turn_rows():
            words = rows[:].bitcast(F32)
            for u in range(2):
                nc.tensor.transpose(bank[7][:, cols(u)], words[:, u : 2 * P : 2], ident_f32[:])
            nc.tensor.transpose(bank[7][:, 2 * P : 2 * P + P // 2].bitcast(BF16), rows[:, 0:P], ident_bf16[:])

        def spread_rows():
            halves = bank[7][:, 0 : 2 * P].bitcast(BF16).rearrange("p (u r e) -> p r u e", u=2, e=2)
            nc.vector.tensor_copy(
                out=weight_sb[:].rearrange("p g (u e) -> p g u e", e=2), in_=halves[:, 0:PASSES, :, :]
            )
            turned = bank[7][:, 2 * P : 2 * P + P // 2].bitcast(BF16)
            nc.vector.tensor_copy(out=comparison_sb[:], in_=turned[:, PASSES : PASSES + TILES])

        def interleave_prec(engine, half):
            interleave(engine, prec_il[:, cols(half, F // 2), :], prec_raw[:, :, cols(half, F // 2)])

        def quantize_prec():
            quantize(prec_codes[:], prec_scales[:], prec_il[:])

        def own_lane(codes):
            return codes[:].bitcast(U8).rearrange("p (a r) -> p a r", r=4 * PACK)[:, :, 0 : 4 * PACK : PACK + 1]

        def split_prec():
            nc.vector.tensor_copy(out=own_lane(prec_own), in_=own_lane(prec_codes))

        def clear_lanes():
            nc.gpsimd.memset(own_lane(prec_codes), 0)

        def xw(g):
            return ring[(g + 1) % 3][:].rearrange("p (t f) -> p t f", t=PACK)

        def ce_il(g):
            return ring[g % 3][:].bitcast(BF16).rearrange("p (w t) -> p w t", t=PACK)

        def d_il(g):
            return ce_il(2)[:, 0:K_PASS, :] if g == 0 else d_tiles[g % 2][:]

        def turn_x(g, half):
            words = x_sb[g % X_BUFS][:].rearrange("p t f -> p (t f)").bitcast(F32)
            for tt in range(2):
                first = (2 * half + tt) * (F // 2)
                for u in range(2):
                    nc.tensor.transpose(
                        turn_banks[half][:, cols(2 * u + tt)],
                        words[:, first + u : first + F // 2 : 2],
                        ident_f32[:],
                    )

        def centre_x(g, half):
            nc.vector.tensor_tensor(
                out=d_il(g)[:, cols(half, 2 * P), :].rearrange("p r (u e) -> p r u e", e=2),
                in0=turn_banks[half][:].bitcast(BF16).rearrange("p (u r e) -> p r u e", u=2, e=2),
                in1=centre_rows[:].rearrange("p r (u e) -> p r u e", e=2),
                op=ALU.subtract,
            )

        def quantize_d(g):
            quantize(d_codes[g % 2][:], d_scales[g % 2][:], d_il(g))

        def stage_one(g, c):
            for t in range(PACK):
                for part, codes in enumerate((prec_codes, prec_own)):
                    mx(
                        q_bank(g, c)[:, cols(t)],
                        d_codes[g % 2][:, cols(t)],
                        d_scales[g % 2][:, cols(t)],
                        codes[:, cols(c)],
                        prec_scales[:, cols(c)],
                        part == 0,
                        part == 1,
                    )

        def weigh_x(g, engine, t0, t1):
            for t in range(t0, t1):
                out, in_, factor = xw(g)[:, t, :], x_sb[g % X_BUFS][:, t, :], weight_sb[:, g, t : t + 1]
                if engine == "scalar":
                    nc.scalar.activation(out=out, in_=in_, func=ACT.Copy, scale=factor)
                else:
                    nc.gpsimd.tensor_scalar(
                        out=out, in0=in_, scalar1=factor, scalar2=0.0, op0=ALU.mult, op1=ALU.add
                    )

        def make_c(g, c):
            nc.vector.tensor_tensor(
                out=ce_il(g)[:, cols(c), :].rearrange("p (c i) t -> p c t i", i=2),
                in0=q_bank(g, c)[:].rearrange("p (t c i) -> p c t i", t=PACK, i=2),
                in1=xw(g)[:, :, cols(c)].rearrange("p t (c i) -> p c t i", i=2),
                op=ALU.mult,
            )

        def quantize_ce(g):
            quantize(ce_codes[g][:], ce_scales[g][:], ce_il(g))

        def interleave_early(g):
            interleave("scalar", ce_il(g)[:, F : F + HALF, :], g_raw[g % G_BUFS][:, :, 0:HALF])

        def interleave_late(g, m0, m1):
            nc.scalar.copy(
                out=gl_il[g // 4][:, m0 - TILES // 2 : m1 - TILES // 2, g % 4, :, :].rearrange(
                    "p m (c i) t -> p m c t i", i=RUN
                ),
                in_=g_raw[g % G_BUFS][:, :, m0 * P : m1 * P].rearrange(
                    "p t (m c i) -> p m c t i", c=P // RUN, i=RUN
                ),
            )

        def quantize_late(m0, m1, half):
            late = slice(m0 - TILES // 2, m1 - TILES // 2)
            quantize(
                gl_codes[half][:, late, :, :].rearrange("p m g l -> p (m g l)"),
                gl_scales[half][:, late, :, :].rearrange("p m g l -> p (m g l)"),
                gl_il[half][:, late, :, :, :].rearrange("p m g l t -> p (m g l) t"),
            )

        def stage_two(m, g0, g1):
            for g in range(g0, g1):
                if m < TILES // 2:
                    codes, scales = ce_codes[g][:, cols(PACK + m)], ce_scales[g][:, cols(PACK + m)]
                else:
                    late = m - TILES // 2
                    codes, scales = gl_codes[g // 4][:, late, g % 4, :], gl_scales[g // 4][:, late, g % 4, :]
                mx(bank[m][:], codes, scales, ce_codes[g][:, 0:F], ce_scales[g][:, 0:F], g == 0, g == PASSES - 1)

        def scale_out(m):
            nc.vector.scalar_tensor_tensor(
                out=y_sb[:, m, :],
                in0=bank[m][:],
                scalar=comparison_sb[:, m : m + 1],
                in1=penalty_sb[:],
                op0=ALU.mult,
                op1=ALU.mult,
            )

        def store_y(m0, m1):
            nc.sync.dma_start(out=y_hbm[:, m0:m1, :], in_=y_sb[:, m0:m1, :])

        def scale_out_rounded(m):
            for u in range(2):
                nc.vector.scalar_tensor_tensor(
                    out=y_bf[m][:, cols(u, F // 2)].rearrange("p (q e) -> p q e", e=2),
                    in0=bank[m][:].rearrange("p (q u e) -> p u q e", u=2, e=2)[:, u, :, :],
                    scalar=comparison_sb[:, m : m + 1],
                    in1=penalty_sb[:].rearrange("p (q u e) -> p u q e", u=2, e=2)[:, u, :, :],
                    op0=ALU.mult,
                    op1=ALU.mult,
                )

        def round_y(engine, m):
            copy_on(
                engine,
                y_bf[m][:].rearrange("p (u q e) -> p u q e", u=2, e=2),
                y_sb[:, m, :].rearrange("p (q u e) -> p u q e", u=2, e=2),
            )

        def turn_y(ms, b):
            for i, m in enumerate(ms):
                words = y_bf[m][:].bitcast(F32)
                for u in range(2):
                    nc.tensor.transpose(bank[b][:, cols(2 * u + i)], words[:, cols(u)], ident_f32[:])

        def gather_y(engine, ms, b):
            width = len(ms) * P
            first = (ms[0] % 4) * P
            copy_on(
                engine,
                flat(y_il[ms[0] // 4][:, first : first + width, :]).bitcast(F32).rearrange("p (r u) -> p r u", u=2),
                bank[b][:].rearrange("p (u r) -> p r u", u=2)[:, 0:width, :],
            )

        def quantize_y(ms):
            width = len(ms) * P
            first = (ms[0] % 4) * P
            span = slice(ms[0] * P, ms[0] * P + width)
            quantize(y_codes[:, span], y_scales[:, span], y_il[ms[0] // 4][:, first : first + width, :])

        def store_words(m0, m1):
            span = slice(m0 * P, m1 * P)
            nc.sync.dma_start(out=words_hbm[:, span], in_=y_codes[:, span].bitcast(I32))

        def store_scales():
            scale_words = y_scales[:].bitcast(I32)
            for quad in range(4):
                queue = nc.scalar if quad % 2 == 0 else nc.sync
                queue.dma_start(
                    out=scales_hbm[4 * quad : 4 * quad + 4, :], in_=scale_words[32 * quad : 32 * quad + 4, :]
                )

        ctx.enter_context(tc.manual_schedule())
        load_prec(1)
        load_x(0, 0, 2)
        load_prec(0)
        load_x(0, 2, 4)
        constants()
        load_x(1)
        load_groups(0)
        load_x(2)
        load_groups(1)
        load_x(3)
        load_groups(2)

        turn_x(0, 0)
        turn_rows()
        turn_x(0, 1)
        interleave_prec("vector", 1)
        interleave_prec("scalar", 0)
        repeat_centre()
        centre_x(0, 0)
        quantize_prec()
        spread_rows()
        weigh_x(0, "scalar", 0, 4)
        turn_x(1, 0)
        split_prec()
        clear_lanes()
        centre_x(0, 1)
        turn_x(1, 1)
        quantize_d(0)
        centre_x(1, 0)
        centre_x(1, 1)
        stage_one(0, 0)
        stage_one(0, 1)
        turn_x(2, 0)
        turn_x(2, 1)
        stage_one(0, 2)
        stage_one(0, 3)

        last = PASSES - 1

        def side_work(s):
            interleave_early(s)
            if s < last:
                weigh_x(s + 1, "gpsimd", 0, 3)
                weigh_x(s + 1, "scalar", 3, 4)
            interleave_late(s, 4, 8 if s < last - 1 else 6)

        def next_loads(s):
            if s + 4 <= last:
                load_x(s + 4)
            if s + 3 <= last:
                load_groups(s + 3)
            if s == 4:
                load_penalty()

        side_work(0)
        make_c(0, 0)
        make_c(0, 1)
        centre_x(2, 0)
        centre_x(2, 1)
        quantize_d(1)
        stage_one(1, 0)
        stage_one(1, 1)
        turn_x(3, 0)
        turn_x(3, 1)
        make_c(0, 2)
        make_c(0, 3)
        quantize_d(2)
        quantize_ce(0)
        next_loads(0)

        for s in range(1, last - 1):
            stage_two(0, s - 1, s)
            stage_two(1, s - 1, s)
            side_work(s)
            make_c(s, 0)
            make_c(s, 1)
            stage_one(s, 2)
            stage_one(s, 3)
            centre_x(s + 2, 0)
            centre_x(s + 2, 1)
            stage_two(2, s - 1, s)
            stage_two(3, s - 1, s)
            if s + 3 <= last:
                turn_x(s + 3, 0)
                turn_x(s + 3, 1)
            else:
                stage_one(s + 1, 2)
                stage_one(s + 1, 3)
            make_c(s, 2)
            make_c(s, 3)
            stage_one(s + 1, 0)
            stage_one(s + 1, 1)
            quantize_d(s + 2)
            if s == last - 2:
                quantize_late(4, 5, 0)
            quantize_ce(s)
            next_loads(s)

        s = last - 1
        for m in range(4):
            stage_two(m, s - 1, s)
        side_work(s)
        make_c(s, 0)
        make_c(s, 1)
        stage_one(last, 0)
        stage_one(last, 1)
        make_c(s, 2)
        make_c(s, 3)
        stage_two(4, 0, 4)
        quantize_late(5, 6, 0)
        stage_two(5, 0, 4)
        quantize_ce(s)

        stage_two(0, s, last)
        stage_two(1, s, last)
        side_work(last)
        interleave_late(s, 6, 8)
        interleave_late(last, 6, 8)
        make_c(last, 0)
        make_c(last, 1)
        stage_one(last, 2)
        stage_one(last, 3)
        quantize_late(6, 7, 0)
        stage_two(2, s, last)
        stage_two(3, s, last)
        make_c(last, 2)
        make_c(last, 3)
        stage_two(6, 0, 4)
        quantize_late(7, 8, 0)
        stage_two(7, 0, 3)
        quantize_ce(last)

        for m in range(4):
            stage_two(m, last, PASSES)
        quantize_late(4, 6, 1)
        stage_two(7, 3, 4)
        stage_two(4, 4, 8)
        scale_out(0)
        round_y("scalar", 0)
        scale_out(1)
        round_y("scalar", 1)
        store_y(0, 2)
        quantize_late(6, 8, 1)
        stage_two(5, 4, 8)
        turn_y([0, 1], 0)
        stage_two(6, 4, 8)
        stage_two(7, 4, 8)
        scale_out(2)
        round_y("gpsimd", 2)
        gather_y("scalar", [0, 1], 0)
        scale_out(3)
        round_y("scalar", 3)
        store_y(2, 4)
        scale_out(4)
        round_y("gpsimd", 4)
        scale_out(5)
        round_y("scalar", 5)
        store_y(4, 6)
        scale_out(6)
        round_y("gpsimd", 6)
        store_y(6, 7)
        turn_y([2, 3], 1)
        scale_out_rounded(7)
        gather_y("scalar", [2, 3], 1)
        turn_y([4, 5], 2)
        turn_y([6, 7], 3)
        scale_out(7)
        store_y(7, 8)
        gather_y("scalar", [4, 5], 2)
        quantize_y([0, 1, 2, 3])
        store_words(0, 4)
        gather_y("scalar", [6, 7], 3)
        quantize_y([4, 5])
        store_words(4, 6)
        quantize_y([6, 7])
        store_words(6, 8)
        store_scales()
